import numpy as np
CORES = [0,8,16,24,128,136,144,152,256,264,272,280,384,392,400,408]
N = 16
GROUPS = [[0,1,2,3,4,5,6,7],[8,9,10,11,12,13,14,15]]
def setup_inputs(rng):
    return {"x": rng.standard_normal((N, 128, 64), dtype=np.float32)}
def reference(x):
    y = np.empty((N, 128, 64), x.dtype)
    for g in GROUPS:
        n = len(g); b = x.shape[2] // n
        for i, r in enumerate(g):
            y[r] = np.concatenate([x[s][:, i * b:(i + 1) * b] for s in g], axis=1)
    return {"y": y}

@@ -1,0 +1,87 @@
+import concourse.bass as bass
+
+WIDTH = 64
+SCRATCH = {
+    "send": ("sbuf", [128, WIDTH], "float32"),
+    "land": ("sbuf", [128, WIDTH], "float32"),
+    "relay": ("sbuf", [128, 8], "float32"),
+}
+SEMAPHORES = ["loaded", "own", "got", "arrived", "sent", "stored"]
+
+HELPERS = (2, 3, 6, 7)
+HAND_MASKS = (0x000F, 0x00F0, 0x0F00, 0xF000)
+DIRECT_MASKS = (0x000F, 0x0030, 0x00C0)
+OFF_CHIP = 0x00FF
+
+
+def engines(mask):
+    return bin(mask).count("1")
+
+
+def plan(T, topo, rank):
+    group = [grp for grp in T.tables["GROUPS"] if rank in grp][0]
+    src = T.cores[rank]
+    near, far = [], []
+    for j, r in enumerate(group):
+        if r == rank:
+            continue
+        dst = T.cores[r]
+        kind = (topo.host(dst) != topo.host(src), topo.chip(dst) ^ topo.chip(src))
+        (near if topo.may_write(src, dst) else far).append((kind, j, dst))
+    near.sort()
+    far.sort()
+    direct = [(j, dst, DIRECT_MASKS[k]) for k, (kind, j, dst) in enumerate(near)]
+    relayed = [(j, dst, src + HELPERS[k], HAND_MASKS[k]) for k, (kind, j, dst) in enumerate(far)]
+    return group.index(rank), WIDTH // len(group), direct, relayed
+
+
+def transfer(topo, core, dst, mask, sem, src_ap, dst_ap):
+    rid, pid = topo.addr(dst, core)
+    return bass.RemoteDMATransfer(dst_ids=[bass.DstId(rid=rid, pnc=pid)], dma_engine_mask=mask, remote_sem=sem,
+                                  src=src_ap, dst=dst_ap)
+
+
+def helper_program(g, core, T, topo):
+    rank = T.rank_of(core - core % 8)
+    if rank is None or core % 8 not in HELPERS:
+        return
+    i, b, direct, relayed = plan(T, topo, rank)
+    for j, dst, helper, mask in relayed:
+        if helper != core:
+            continue
+        g.wait_ge(T.sem.got, engines(mask))
+        rid, pid = topo.addr(dst, core)
+        g.remote_dma(T.land[:, i * b:(i + 1) * b], T.relay[:, 0:b], T.sem.arrived, T.sem.sent, pid, rid, OFF_CHIP)
+        g.wait_ge(T.sem.sent, engines(OFF_CHIP))
+
+
+def rank_program(g, core, T, topo):
+    rank = T.rank_of(core)
+    if rank is None:
+        helper_program(g, core, T, topo)
+        return
+    i, b, direct, relayed = plan(T, topo, rank)
+    mine = T.land[:, i * b:(i + 1) * b]
+
+    g.dma_start(T.send[:], T.x[:]).then_inc(T.sem.loaded, 16)
+    g.dma_start(mine, T.x[:, i * b:(i + 1) * b]).then_inc(T.sem.own, 16)
+    g.wait_ge(T.sem.loaded, 16)
+
+    g.remote_dma_fused([transfer(topo, core, helper, mask, T.sem.got, T.send[:, j * b:(j + 1) * b], T.relay[:, 0:b])
+                        for j, dst, helper, mask in relayed], local_sem=T.sem.sent)
+    g.remote_dma_fused([transfer(topo, core, dst, mask, T.sem.arrived, T.send[:, j * b:(j + 1) * b], mine)
+                        for j, dst, mask in direct], local_sem=T.sem.sent)
+
+    expect = 0
+    group = [grp for grp in T.tables["GROUPS"] if rank in grp][0]
+    for r in group:
+        if r == rank:
+            continue
+        si, sb, sdirect, srelayed = plan(T, topo, r)
+        expect += sum(engines(mask) for j, dst, mask in sdirect if dst == core)
+        expect += sum(engines(OFF_CHIP) for j, dst, helper, mask in srelayed if dst == core)
+    g.wait_ge(T.sem.own, 16)
+    g.wait_ge(T.sem.arrived, expect)
+    g.dma_start(T.y[:], T.land[:]).then_inc(T.sem.stored, 16)
+    g.wait_ge(T.sem.sent, sum(engines(m) for j, d, m in direct) + sum(engines(m) for j, d, h, m in relayed))
+    g.wait_ge(T.sem.stored, 16)

@@ -8,10 +8,17 @@ SCRATCH = {
 }
 SEMAPHORES = ["loaded", "own", "got", "arrived", "sent", "stored"]
 
-HELPERS = (2, 3, 6, 7)
-HAND_MASKS = (0x000F, 0x00F0, 0x0F00, 0xF000)
-DIRECT_MASKS = (0x000F, 0x0030, 0x00C0)
 OFF_CHIP = 0x00FF
+ROUTE = {
+    (False, 1): (2, 0, 0x000F),
+    (False, 3): (3, 0, 0x00F0),
+    (True, 1): (6, 0, 0x0F00),
+    (True, 3): (7, 0, 0xF000),
+    (False, 2): (0, 1, 0x000F),
+    (True, 0): (0, 1, 0x00F0),
+    (True, 2): (0, 2, 0x00FF),
+}
+CALLS = 1 + max(call for who, call, mask in ROUTE.values())
 
 
 def engines(mask):
@@ -21,18 +28,14 @@ def engines(mask):
 def plan(T, topo, rank):
     group = [grp for grp in T.tables["GROUPS"] if rank in grp][0]
     src = T.cores[rank]
-    near, far = [], []
+    jobs = []
     for j, r in enumerate(group):
         if r == rank:
             continue
         dst = T.cores[r]
-        kind = (topo.host(dst) != topo.host(src), topo.chip(dst) ^ topo.chip(src))
-        (near if topo.may_write(src, dst) else far).append((kind, j, dst))
-    near.sort()
-    far.sort()
-    direct = [(j, dst, DIRECT_MASKS[k]) for k, (kind, j, dst) in enumerate(near)]
-    relayed = [(j, dst, src + HELPERS[k], HAND_MASKS[k]) for k, (kind, j, dst) in enumerate(far)]
-    return group.index(rank), WIDTH // len(group), direct, relayed
+        who, call, mask = ROUTE[(topo.host(dst) != topo.host(src), topo.chip(dst) ^ topo.chip(src))]
+        jobs.append((j, dst, src + who if who else None, call, mask))
+    return group.index(rank), WIDTH // len(group), jobs
 
 
 def transfer(topo, core, dst, mask, sem, src_ap, dst_ap):
@@ -43,10 +46,10 @@ def transfer(topo, core, dst, mask, sem, src_ap, dst_ap):
 
 def helper_program(g, core, T, topo):
     rank = T.rank_of(core - core % 8)
-    if rank is None or core % 8 not in HELPERS:
+    if rank is None:
         return
-    i, b, direct, relayed = plan(T, topo, rank)
-    for j, dst, helper, mask in relayed:
+    i, b, jobs = plan(T, topo, rank)
+    for j, dst, helper, call, mask in jobs:
         if helper != core:
             continue
         g.wait_ge(T.sem.got, engines(mask))
@@ -60,28 +63,26 @@ def rank_program(g, core, T, topo):
     if rank is None:
         helper_program(g, core, T, topo)
         return
-    i, b, direct, relayed = plan(T, topo, rank)
+    i, b, jobs = plan(T, topo, rank)
     mine = T.land[:, i * b:(i + 1) * b]
 
     g.dma_start(T.send[:], T.x[:]).then_inc(T.sem.loaded, 16)
     g.dma_start(mine, T.x[:, i * b:(i + 1) * b]).then_inc(T.sem.own, 16)
     g.wait_ge(T.sem.loaded, 16)
 
-    g.remote_dma_fused([transfer(topo, core, helper, mask, T.sem.got, T.send[:, j * b:(j + 1) * b], T.relay[:, 0:b])
-                        for j, dst, helper, mask in relayed], local_sem=T.sem.sent)
-    g.remote_dma_fused([transfer(topo, core, dst, mask, T.sem.arrived, T.send[:, j * b:(j + 1) * b], mine)
-                        for j, dst, mask in direct], local_sem=T.sem.sent)
+    for c in range(CALLS):
+        g.remote_dma_fused(
+            [transfer(topo, core, helper, mask, T.sem.got, T.send[:, j * b:(j + 1) * b], T.relay[:, 0:b]) if helper
+             else transfer(topo, core, dst, mask, T.sem.arrived, T.send[:, j * b:(j + 1) * b], mine)
+             for j, dst, helper, call, mask in jobs if call == c], local_sem=T.sem.sent)
 
     expect = 0
-    group = [grp for grp in T.tables["GROUPS"] if rank in grp][0]
-    for r in group:
-        if r == rank:
-            continue
-        si, sb, sdirect, srelayed = plan(T, topo, r)
-        expect += sum(engines(mask) for j, dst, mask in sdirect if dst == core)
-        expect += sum(engines(OFF_CHIP) for j, dst, helper, mask in srelayed if dst == core)
+    for r in [grp for grp in T.tables["GROUPS"] if rank in grp][0]:
+        if r != rank:
+            expect += sum(engines(OFF_CHIP if helper else mask)
+                          for j, dst, helper, call, mask in plan(T, topo, r)[2] if dst == core)
     g.wait_ge(T.sem.own, 16)
     g.wait_ge(T.sem.arrived, expect)
     g.dma_start(T.y[:], T.land[:]).then_inc(T.sem.stored, 16)
-    g.wait_ge(T.sem.sent, sum(engines(m) for j, d, m in direct) + sum(engines(m) for j, d, h, m in relayed))
+    g.wait_ge(T.sem.sent, sum(engines(mask) for j, dst, helper, call, mask in jobs))
     g.wait_ge(T.sem.stored, 16)

import concourse.bass as bass

WIDTH = 64
SCRATCH = {
    "send": ("sbuf", [128, WIDTH], "float32"),
    "land": ("sbuf", [128, WIDTH], "float32"),
    "relay": ("sbuf", [128, 8], "float32"),
}
SEMAPHORES = ["loaded", "own", "got", "arrived", "sent", "stored"]

OFF_CHIP = 0x00FF
ROUTE = {
    (False, 1): (2, 0, 0x000F),
    (False, 3): (3, 0, 0x00F0),
    (True, 1): (6, 0, 0x0F00),
    (True, 3): (7, 0, 0xF000),
    (False, 2): (0, 1, 0x000F),
    (True, 0): (0, 1, 0x00F0),
    (True, 2): (0, 2, 0x00FF),
}
CALLS = 1 + max(call for who, call, mask in ROUTE.values())


def engines(mask):
    return bin(mask).count("1")


def plan(T, topo, rank):
    group = [grp for grp in T.tables["GROUPS"] if rank in grp][0]
    src = T.cores[rank]
    jobs = []
    for j, r in enumerate(group):
        if r == rank:
            continue
        dst = T.cores[r]
        who, call, mask = ROUTE[(topo.host(dst) != topo.host(src), topo.chip(dst) ^ topo.chip(src))]
        jobs.append((j, dst, src + who if who else None, call, mask))
    return group.index(rank), WIDTH // len(group), jobs


def transfer(topo, core, dst, mask, sem, src_ap, dst_ap):
    rid, pid = topo.addr(dst, core)
    return bass.RemoteDMATransfer(dst_ids=[bass.DstId(rid=rid, pnc=pid)], dma_engine_mask=mask, remote_sem=sem,
                                  src=src_ap, dst=dst_ap)


def helper_program(g, core, T, topo):
    rank = T.rank_of(core - core % 8)
    if rank is None:
        return
    i, b, jobs = plan(T, topo, rank)
    for j, dst, helper, call, mask in jobs:
        if helper != core:
            continue
        g.wait_ge(T.sem.got, engines(mask))
        rid, pid = topo.addr(dst, core)
        g.remote_dma(T.land[:, i * b:(i + 1) * b], T.relay[:, 0:b], T.sem.arrived, T.sem.sent, pid, rid, OFF_CHIP)
        g.wait_ge(T.sem.sent, engines(OFF_CHIP))


def rank_program(g, core, T, topo):
    rank = T.rank_of(core)
    if rank is None:
        helper_program(g, core, T, topo)
        return
    i, b, jobs = plan(T, topo, rank)
    mine = T.land[:, i * b:(i + 1) * b]

    g.dma_start(T.send[:], T.x[:]).then_inc(T.sem.loaded, 16)
    g.dma_start(mine, T.x[:, i * b:(i + 1) * b]).then_inc(T.sem.own, 16)
    g.wait_ge(T.sem.loaded, 16)

    for c in range(CALLS):
        g.remote_dma_fused(
            [transfer(topo, core, helper, mask, T.sem.got, T.send[:, j * b:(j + 1) * b], T.relay[:, 0:b]) if helper
             else transfer(topo, core, dst, mask, T.sem.arrived, T.send[:, j * b:(j + 1) * b], mine)
             for j, dst, helper, call, mask in jobs if call == c], local_sem=T.sem.sent)

    expect = 0
    for r in [grp for grp in T.tables["GROUPS"] if rank in grp][0]:
        if r != rank:
            expect += sum(engines(OFF_CHIP if helper else mask)
                          for j, dst, helper, call, mask in plan(T, topo, r)[2] if dst == core)
    g.wait_ge(T.sem.own, 16)
    g.wait_ge(T.sem.arrived, expect)
    g.dma_start(T.y[:], T.land[:]).then_inc(T.sem.stored, 16)
    g.wait_ge(T.sem.sent, sum(engines(mask) for j, dst, helper, call, mask in jobs))
    g.wait_ge(T.sem.stored, 16)
